import numpy as np
CORES = [6,22,38,54,70,86,102,118]
N = 8
ROOT = 2
WIDTHS = [5,17,2,30,11,64,9,23]
XW = 64
def setup_inputs(rng):
    return {"x": rng.standard_normal((N, 128, XW), dtype=np.float32)}
def reference(x):
    g = np.concatenate([x[r][:, :WIDTHS[r]] for r in range(N)], axis=1)
    y = np.full((N, 128, g.shape[1]), np.nan, x.dtype)
    y[ROOT] = g
    return {"y": y}

SCRATCH = {
    "land": ("sbuf", [128, 161], "float32"),
}
SEMAPHORES = ["loaded", "read", "arrived", "stored"]


def rank_program(g, core, T, topo):
    rank = T.rank_of(core)
    if rank is None:
        return
    widths = T.tables["WIDTHS"]
    root_rank = 2
    root = T.cores[root_rank]
    off = sum(widths[:rank])
    w = widths[rank]
    total = sum(widths)

    g.dma_start(T.land[:, off:off + w], T.x[:, 0:w]).then_inc(T.sem.loaded, 16)

    if core != root:
        rid, pid, _se = topo.addr(root)
        mask = topo.mask(core, root)
        g.wait_ge(T.sem.loaded, 16)
        g.remote_dma(T.land[:, off:off + w], T.land[:, off:off + w], T.sem.arrived, T.sem.read, pid, rid, mask)
        g.wait_ge(T.sem.read, 8)
        return

    g.wait_ge(T.sem.arrived, 8 * (len(widths) - 1))
    g.wait_ge(T.sem.loaded, 16)
    g.dma_start(T.y[:, 0:total], T.land[:, 0:total]).then_inc(T.sem.stored, 16)
    g.wait_ge(T.sem.stored, 16)
